import numpy as np, ml_dtypes
CORES = [2,3,42,43,82,83,122,123]
N = 8
QP = 256
WID = [256,32,128,256,256,160,128,64]
def setup_inputs(rng):
    return {"q": rng.standard_normal((N, 128, QP), dtype=np.float32).astype(ml_dtypes.bfloat16), "k": rng.standard_normal((N, 128, 128), dtype=np.float32).astype(ml_dtypes.bfloat16), "v": rng.standard_normal((N, 128, 128), dtype=np.float32).astype(ml_dtypes.bfloat16)}
def setup_inputs_big(rng):
    d = setup_inputs(rng)
    for k in ("q", "k", "v"): d[k] = (d[k].astype(np.float32) * 1024.0).astype(d[k].dtype)
    return d
def setup_inputs_small(rng):
    d = setup_inputs(rng)
    for k in ("q", "k", "v"): d[k] = (d[k].astype(np.float32) * (1 / 1024.0)).astype(d[k].dtype)
    return d
def setup_inputs_apart(rng):
    d = setup_inputs(rng)
    f = (10.0 ** rng.permutation(np.linspace(-1.5, 1.5, N))).astype(np.float32).reshape(N, 1, 1)
    for k in ("q", "k", "v"): d[k] = (d[k].astype(np.float32) * f).astype(d[k].dtype)
    return d
def whole(q, k, v):
    Q, K, V = q.astype(np.float64), k.astype(np.float64), v.astype(np.float64)
    y = np.zeros((N, 128, QP))
    for r in range(N):
        S = [K[j].T @ Q[r] for j in range(N)]
        m = np.max([s.max(axis=0) for s in S], axis=0)
        y[r] = sum(V[j].T @ np.maximum(S[j] - 0.5 * m, 0.0) for j in range(N))
    return {"y": y.astype(ml_dtypes.bfloat16)}
def reference(q, k, v):
    o = whole(q, k, v)["y"].copy()
    for r in range(N):
        o[r][:, WID[r]:] = np.nan
    return {"y": o}

@@ -1,0 +1,196 @@
+from concourse.bass import DstId, RemoteDMATransfer
+from concourse.mybir import AluOpType
+
+B = 128
+SCRATCH = {
+    "KV": ("sbuf", [128, 16 * B], "bfloat16"),
+    "Q": ("sbuf", [128, 256], "bfloat16"),
+    "R": ("sbuf", [128, 256], "bfloat16"),
+    "TR": ("sbuf", [128, 256], "bfloat16"),
+    "MT": ("sbuf", [128, 2], "bfloat16"),
+    "IDA": ("sbuf", [128, 129], "bfloat16"),
+    "IDD": ("dram", [129, 128], "bfloat16"),
+    "ID": ("sbuf", [128, 128], "bfloat16"),
+    "SEL": ("sbuf", [128, 512], "bfloat16"),
+    "MROW": ("sbuf", [128, 128], "bfloat16"),
+    "HB": ("sbuf", [128, 256], "bfloat16"),
+    "NHB": ("sbuf", [128, 256], "bfloat16"),
+    "P": ("sbuf", [128, 8 * 256], "bfloat16"),
+    "YS": ("sbuf", [128, 256], "bfloat16"),
+    "S": ("psum", [128, 8 * 256], "float32"),
+    "X0": ("psum", [128, 512], "float32"),
+    "X1": ("psum", [128, 512], "float32"),
+    "X2": ("psum", [128, 512], "float32"),
+    "X3": ("psum", [128, 512], "float32"),
+}
+SEMAPHORES = ["ld_k", "ld_v", "ld_q", "id1", "id2", "mt", "kd", "vd", "kf", "vf", "sent", "ps", "vs", "st"]
+
+KCOL = [0, 2, 4, 5, 6, 10, 11, 12]
+VCOL = [1, 3, 7, 8, 9, 13, 14, 15]
+
+
+def _blk(t, c, n=1):
+    return t[:, c * B:(c + n) * B]
+
+
+def _bits(m):
+    return bin(m).count("1")
+
+
+def rank_program(g, core, T, topo):
+    rank = T.rank_of(core)
+    if rank is None:
+        return
+    W = T.tables["WID"][rank]
+    nb = (W + B - 1) // B
+    sem = T.sem
+    KV = T.KV
+
+    chips, members = [], {}
+    for c in T.cores:
+        ch = topo.chip(c)
+        if ch not in members:
+            chips.append(ch)
+            members[ch] = []
+        members[ch].append(c)
+    nch = len(chips)
+    ci = chips.index(topo.chip(core))
+    pos = members[chips[ci]].index(core)
+    mate = members[chips[ci]][1 - pos]
+    far = [members[chips[(ci + w) % nch]][pos] for w in range(1, nch)]
+    off_mask = topo.mask(core, mate)
+    for d in far:
+        assert topo.may_write(core, d)
+        off_mask &= topo.mask(core, d)
+    on_mask = topo.mask(core, mate) & ~off_mask
+    n_off, n_on = _bits(off_mask), _bits(on_mask)
+    far_ids = []
+    for d in far:
+        rid, pid, _se = topo.addr(d)
+        far_ids.append(DstId(rid=rid, pnc=pid))
+    m_rid, m_pid, _se = topo.addr(mate)
+
+    g.sync.dma_start(_blk(KV, KCOL[0]), T.k[:]).then_inc(sem.ld_k, 16)
+    g.scalar.dma_start(_blk(KV, VCOL[0]), T.v[:]).then_inc(sem.ld_v, 16)
+    g.sync.dma_start(T.Q[:, 0:nb * B], T.q[:, 0:nb * B]).then_inc(sem.ld_q, 16)
+
+    g.wait_ge(sem.ld_k, 16)
+    g.remote_dma_fused([RemoteDMATransfer(
+        dst_ids=far_ids, dma_engine_mask=off_mask, remote_sem=sem.kd,
+        srcs=[_blk(KV, KCOL[0])], dsts=[_blk(KV, KCOL[2] + w) for w in range(nch - 1)], alu_op=0)],
+        local_sem=sem.sent)
+    g.wait_ge(sem.ld_v, 16)
+    g.remote_dma_fused([RemoteDMATransfer(
+        dst_ids=far_ids, dma_engine_mask=off_mask, remote_sem=sem.vd,
+        srcs=[_blk(KV, VCOL[0])], dsts=[_blk(KV, VCOL[2] + w) for w in range(nch - 1)], alu_op=0)],
+        local_sem=sem.sent)
+    g.remote_dma(_blk(KV, KCOL[1], 2), _blk(KV, KCOL[0], 2), sem.mt, sem.sent, m_pid, m_rid, on_mask)
+    n_far = (nch - 1) * n_off
+    g.wait_ge(sem.kd, n_far)
+    g.remote_dma(_blk(KV, KCOL[5], 3), _blk(KV, KCOL[2], 3), sem.kf, sem.sent, m_pid, m_rid, on_mask)
+    g.wait_ge(sem.vd, n_far)
+    g.remote_dma(_blk(KV, VCOL[5], 3), _blk(KV, VCOL[2], 3), sem.vf, sem.sent, m_pid, m_rid, on_mask)
+    g.wait_ge(sem.sent, 2 * n_off + 3 * n_on)
+
+    ve, pe = g.vector, g.tensor
+    nv, npe = [0], [0]
+
+    def V(ins):
+        ins.then_inc(sem.vs, 1)
+        nv[0] += 1
+        return nv[0]
+
+    def MM(out, lhsT, rhs, start=True, stop=True):
+        pe.matmul(out, lhsT, rhs, start, stop).then_inc(sem.ps, 1)
+        npe[0] += 1
+        return npe[0]
+
+    V(ve.memset(T.IDA[:, 1:129], 0.0))
+    n_ida = V(ve.memset(T.IDA[:, 0:1], 1.0))
+    for c, val in enumerate((0.0, 0.5, 0.0, -0.5)):
+        n1 = V(ve.memset(T.SEL[0:2, c * B:(c + 1) * B], val))
+    ve.wait_ge(sem.vs, n1)
+    for c, val in enumerate((0.5, 0.0, -0.5, 0.0)):
+        n_sel = V(ve.memset(T.SEL[0:1, c * B:(c + 1) * B], val))
+    g.scalar.wait_ge(sem.vs, n_ida)
+    g.scalar.dma_start(T.IDD[:], T.IDA[:]).then_inc(sem.id1, 16)
+    g.scalar.wait_ge(sem.id1, 16)
+    g.scalar.dma_start(T.ID[:], T.IDD[0:128, :]).then_inc(sem.id2, 16)
+
+    X = [T.X0, T.X1, T.X2]
+    k_wait = [[(sem.ld_k, 16), (sem.ld_q, 16)], [(sem.mt, n_on)], [(sem.kd, n_far)], [(sem.kf, n_on)]]
+    v_wait = {0: (sem.ld_v, 16), 1: (sem.mt, n_on), 2: (sem.vd, n_far), 5: (sem.vf, n_on)}
+    groups = [[0], [1], [2, 3, 4], [5, 6, 7]]
+    r_done = {}
+    for gi, grp in enumerate(groups):
+        for s_, n_ in k_wait[gi]:
+            pe.wait_ge(s_, n_)
+        for s in grp:
+            if s >= 3:
+                pe.wait_ge(sem.vs, r_done[s - 3])
+            for b in range(nb):
+                n_st = MM(X[s % 3][:, b * B:(b + 1) * B], _blk(T.Q, b), _blk(KV, KCOL[s]))
+            ve.wait_ge(sem.ps, n_st)
+            if s == 0:
+                r_done[s] = V(ve.tensor_copy(T.R[:, 0:nb * B], X[0][:, 0:nb * B]))
+            else:
+                ve.wait_ge(sem.vs, r_done[s - 1])
+                r_done[s] = V(ve.tensor_tensor(T.R[:, 0:nb * B], X[s % 3][:, 0:nb * B], T.R[:, 0:nb * B],
+                                               AluOpType.max))
+        for s in grp:
+            MM(T.S[:, s * 256:s * 256 + W], _blk(KV, KCOL[s]), T.Q[:, 0:W])
+
+    ve.wait_ge(sem.vs, r_done[7])
+    for b in range(nb):
+        n_t = V(ve.tensor_tensor(T.TR[:, b:64 * nb:nb], T.R[:, b * B:b * B + 64], T.R[:, b * B + 64:(b + 1) * B],
+                                 AluOpType.max))
+    off, ln = 0, 64 * nb
+    while ln > nb:
+        h = ln // 2
+        out = T.MT[:, 0:nb] if h == nb else T.TR[:, off + ln:off + ln + h]
+        ve.wait_ge(sem.vs, n_t)
+        n_t = V(ve.tensor_tensor(out, T.TR[:, off:off + h], T.TR[:, off + h:off + ln], AluOpType.max))
+        off, ln = off + ln, h
+
+    pe.wait_ge(sem.id2, 16)
+    pe.wait_ge(sem.vs, n_t)
+    n_m = MM(T.X0[0:nb, 0:B], T.MT[:, 0:nb], T.ID[:])
+    ve.wait_ge(sem.ps, n_m)
+    n_row = V(ve.tensor_copy(T.MROW[0:nb, :], T.X0[0:nb, 0:B]))
+    pe.wait_ge(sem.vs, n_row)
+    for b in range(nb):
+        wb = min(B, W - b * B)
+        n_h = MM(T.X1[:, b * B:b * B + wb], T.SEL[0:nb, b * B:(b + 1) * B], T.MROW[0:nb, 0:wb])
+    for b in range(nb):
+        wb = min(B, W - b * B)
+        n_nh = MM(T.X2[:, b * B:b * B + wb], T.SEL[0:nb, (2 + b) * B:(3 + b) * B], T.MROW[0:nb, 0:wb])
+    ve.wait_ge(sem.ps, n_h)
+    n_hb = V(ve.tensor_copy(T.HB[:, 0:W], T.X1[:, 0:W]))
+    ve.wait_ge(sem.vs, n_hb)
+    p_done = {}
+    for s in range(8):
+        p_done[s] = V(ve.tensor_tensor(T.P[:, s * 256:s * 256 + W], T.S[:, s * 256:s * 256 + W], T.HB[:, 0:W],
+                                       AluOpType.max))
+        if s == 0:
+            ve.wait_ge(sem.ps, n_nh)
+            n_nhb = V(ve.tensor_copy(T.NHB[:, 0:W], T.X2[:, 0:W]))
+
+    Y = T.X3[:, 0:W]
+    for s in range(8):
+        if s in v_wait:
+            pe.wait_ge(v_wait[s][0], v_wait[s][1])
+        vblk = _blk(KV, VCOL[s])
+        if s == 0:
+            pe.wait_ge(sem.vs, p_done[0])
+            MM(Y, vblk, T.P[:, 0:W], True, False)
+            pe.wait_ge(sem.vs, n_nhb)
+            MM(Y, vblk, T.NHB[:, 0:W], False, False)
+        else:
+            MM(Y, vblk, T.NHB[:, 0:W], False, False)
+            pe.wait_ge(sem.vs, p_done[s])
+            n_y = MM(Y, vblk, T.P[:, s * 256:s * 256 + W], False, s == 7)
+    ve.wait_ge(sem.ps, n_y)
+    n_out = V(ve.tensor_copy(T.YS[:, 0:W], Y))
+    g.sync.wait_ge(sem.vs, n_out)
+    g.sync.dma_start(T.y[:, 0:W], T.YS[:, 0:W]).then_inc(sem.st, 16)
+    g.sync.wait_ge(sem.st, 16)

@@ -11,10 +11,11 @@ SCRATCH = {
     "IDA": ("sbuf", [128, 129], "bfloat16"),
     "IDD": ("dram", [129, 128], "bfloat16"),
     "ID": ("sbuf", [128, 128], "bfloat16"),
-    "SEL": ("sbuf", [128, 512], "bfloat16"),
+    "SEL": ("sbuf", [128, 256], "bfloat16"),
     "MROW": ("sbuf", [128, 128], "bfloat16"),
     "HB": ("sbuf", [128, 256], "bfloat16"),
-    "NHB": ("sbuf", [128, 256], "bfloat16"),
+    "VH": ("sbuf", [128, 128], "bfloat16"),
+    "VL": ("sbuf", [128, 128], "bfloat16"),
     "P": ("sbuf", [128, 8 * 256], "bfloat16"),
     "YS": ("sbuf", [128, 256], "bfloat16"),
     "S": ("psum", [128, 8 * 256], "float32"),
@@ -106,39 +107,66 @@ def rank_program(g, core, T, topo):
         return npe[0]
 
     V(ve.memset(T.IDA[:, 1:129], 0.0))
-    n_ida = V(ve.memset(T.IDA[:, 0:1], 1.0))
-    for c, val in enumerate((0.0, 0.5, 0.0, -0.5)):
+    n_ida = V(ve.memset(T.IDA[:, 0:1], -1.0))
+    for c, val in enumerate((0.0, -0.5)):
         n1 = V(ve.memset(T.SEL[0:2, c * B:(c + 1) * B], val))
     ve.wait_ge(sem.vs, n1)
-    for c, val in enumerate((0.5, 0.0, -0.5, 0.0)):
+    for c, val in enumerate((-0.5, 0.0)):
         n_sel = V(ve.memset(T.SEL[0:1, c * B:(c + 1) * B], val))
     g.scalar.wait_ge(sem.vs, n_ida)
     g.scalar.dma_start(T.IDD[:], T.IDA[:]).then_inc(sem.id1, 16)
     g.scalar.wait_ge(sem.id1, 16)
     g.scalar.dma_start(T.ID[:], T.IDD[0:128, :]).then_inc(sem.id2, 16)
 
-    X = [T.X0, T.X1, T.X2]
-    k_wait = [[(sem.ld_k, 16), (sem.ld_q, 16)], [(sem.mt, n_on)], [(sem.kd, n_far)], [(sem.kf, n_on)]]
-    v_wait = {0: (sem.ld_v, 16), 1: (sem.mt, n_on), 2: (sem.vd, n_far), 5: (sem.vf, n_on)}
-    groups = [[0], [1], [2, 3, 4], [5, 6, 7]]
+    X = [T.X0, T.X1]
     r_done = {}
-    for gi, grp in enumerate(groups):
-        for s_, n_ in k_wait[gi]:
-            pe.wait_ge(s_, n_)
-        for s in grp:
-            if s >= 3:
-                pe.wait_ge(sem.vs, r_done[s - 3])
-            for b in range(nb):
-                n_st = MM(X[s % 3][:, b * B:(b + 1) * B], _blk(T.Q, b), _blk(KV, KCOL[s]))
-            ve.wait_ge(sem.ps, n_st)
-            if s == 0:
-                r_done[s] = V(ve.tensor_copy(T.R[:, 0:nb * B], X[0][:, 0:nb * B]))
-            else:
-                ve.wait_ge(sem.vs, r_done[s - 1])
-                r_done[s] = V(ve.tensor_tensor(T.R[:, 0:nb * B], X[s % 3][:, 0:nb * B], T.R[:, 0:nb * B],
-                                               AluOpType.max))
-        for s in grp:
-            MM(T.S[:, s * 256:s * 256 + W], _blk(KV, KCOL[s]), T.Q[:, 0:W])
+
+    def scores_t(s):
+        if s >= 2:
+            pe.wait_ge(sem.vs, r_done[s - 2])
+        for b in range(nb):
+            n_st = MM(X[s % 2][:, b * B:(b + 1) * B], _blk(T.Q, b), _blk(KV, KCOL[s]))
+        ve.wait_ge(sem.ps, n_st)
+        if s == 0:
+            r_done[s] = V(ve.tensor_copy(T.R[:, 0:nb * B], X[0][:, 0:nb * B]))
+        else:
+            ve.wait_ge(sem.vs, r_done[s - 1])
+            r_done[s] = V(ve.tensor_tensor(T.R[:, 0:nb * B], X[s % 2][:, 0:nb * B], T.R[:, 0:nb * B],
+                                           AluOpType.max))
+
+    def scores(s):
+        MM(T.S[:, s * 256:s * 256 + W], _blk(KV, KCOL[s]), T.Q[:, 0:W])
+
+    def vsum(s):
+        return MM(T.X2[:, 0:B], T.ID[:], _blk(KV, VCOL[s]), s == 0, s == 7)
+
+    pe.wait_ge(sem.ld_k, 16)
+    pe.wait_ge(sem.ld_q, 16)
+    scores_t(0)
+    scores(0)
+    pe.wait_ge(sem.mt, n_on)
+    scores_t(1)
+    scores(1)
+    pe.wait_ge(sem.kd, n_far)
+    for s in (2, 3, 4):
+        scores_t(s)
+    for s in (2, 3, 4):
+        scores(s)
+    pe.wait_ge(sem.id2, 16)
+    pe.wait_ge(sem.ld_v, 16)
+    vsum(0)
+    vsum(1)
+    pe.wait_ge(sem.kf, n_on)
+    for s in (5, 6, 7):
+        scores_t(s)
+    pe.wait_ge(sem.vd, n_far)
+    for s in (2, 3, 4):
+        vsum(s)
+    for s in (5, 6, 7):
+        scores(s)
+    pe.wait_ge(sem.vf, n_on)
+    for s in (5, 6, 7):
+        n_vs = vsum(s)
 
     ve.wait_ge(sem.vs, r_done[7])
     for b in range(nb):
@@ -152,18 +180,18 @@ def rank_program(g, core, T, topo):
         n_t = V(ve.tensor_tensor(out, T.TR[:, off:off + h], T.TR[:, off + h:off + ln], AluOpType.max))
         off, ln = off + ln, h
 
-    pe.wait_ge(sem.id2, 16)
     pe.wait_ge(sem.vs, n_t)
     n_m = MM(T.X0[0:nb, 0:B], T.MT[:, 0:nb], T.ID[:])
+    ve.wait_ge(sem.ps, n_vs)
+    n_vh = V(ve.tensor_copy(T.VH[:], T.X2[:, 0:B]))
     ve.wait_ge(sem.ps, n_m)
     n_row = V(ve.tensor_copy(T.MROW[0:nb, :], T.X0[0:nb, 0:B]))
     pe.wait_ge(sem.vs, n_row)
     for b in range(nb):
         wb = min(B, W - b * B)
         n_h = MM(T.X1[:, b * B:b * B + wb], T.SEL[0:nb, b * B:(b + 1) * B], T.MROW[0:nb, 0:wb])
-    for b in range(nb):
-        wb = min(B, W - b * B)
-        n_nh = MM(T.X2[:, b * B:b * B + wb], T.SEL[0:nb, (2 + b) * B:(3 + b) * B], T.MROW[0:nb, 0:wb])
+    ve.wait_ge(sem.vs, n_vh)
+    n_vl = V(ve.tensor_tensor(T.VL[:], T.X2[:, 0:B], T.VH[:], AluOpType.subtract))
     ve.wait_ge(sem.ps, n_h)
     n_hb = V(ve.tensor_copy(T.HB[:, 0:W], T.X1[:, 0:W]))
     ve.wait_ge(sem.vs, n_hb)
@@ -171,24 +199,14 @@ def rank_program(g, core, T, topo):
     for s in range(8):
         p_done[s] = V(ve.tensor_tensor(T.P[:, s * 256:s * 256 + W], T.S[:, s * 256:s * 256 + W], T.HB[:, 0:W],
                                        AluOpType.max))
-        if s == 0:
-            ve.wait_ge(sem.ps, n_nh)
-            n_nhb = V(ve.tensor_copy(T.NHB[:, 0:W], T.X2[:, 0:W]))
 
     Y = T.X3[:, 0:W]
+    pe.wait_ge(sem.vs, n_hb)
+    MM(Y, T.VH[:], T.HB[:, 0:W], True, False)
+    MM(Y, T.VL[:], T.HB[:, 0:W], False, False)
     for s in range(8):
-        if s in v_wait:
-            pe.wait_ge(v_wait[s][0], v_wait[s][1])
-        vblk = _blk(KV, VCOL[s])
-        if s == 0:
-            pe.wait_ge(sem.vs, p_done[0])
-            MM(Y, vblk, T.P[:, 0:W], True, False)
-            pe.wait_ge(sem.vs, n_nhb)
-            MM(Y, vblk, T.NHB[:, 0:W], False, False)
-        else:
-            MM(Y, vblk, T.NHB[:, 0:W], False, False)
-            pe.wait_ge(sem.vs, p_done[s])
-            n_y = MM(Y, vblk, T.P[:, s * 256:s * 256 + W], False, s == 7)
+        pe.wait_ge(sem.vs, p_done[s])
+        n_y = MM(Y, _blk(KV, VCOL[s]), T.P[:, s * 256:s * 256 + W], False, s == 7)
     ve.wait_ge(sem.ps, n_y)
     n_out = V(ve.tensor_copy(T.YS[:, 0:W], Y))
     g.sync.wait_ge(sem.vs, n_out)

@@ -1,33 +1,30 @@
 from concourse.bass import DstId, RemoteDMATransfer
-from concourse.mybir import AluOpType
+from concourse.mybir import AluOpType, AxisListType, ActivationFunctionType
 
 B = 128
 SCRATCH = {
     "KV": ("sbuf", [128, 16 * B], "bfloat16"),
     "Q": ("sbuf", [128, 256], "bfloat16"),
-    "R": ("sbuf", [128, 256], "bfloat16"),
-    "TR": ("sbuf", [128, 256], "bfloat16"),
-    "MT": ("sbuf", [128, 2], "bfloat16"),
-    "IDA": ("sbuf", [128, 129], "bfloat16"),
-    "IDD": ("dram", [129, 128], "bfloat16"),
+    "ONES": ("sbuf", [128, 128], "bfloat16"),
     "ID": ("sbuf", [128, 128], "bfloat16"),
-    "SEL": ("sbuf", [128, 256], "bfloat16"),
-    "MROW": ("sbuf", [128, 128], "bfloat16"),
-    "HB": ("sbuf", [128, 256], "bfloat16"),
-    "VH": ("sbuf", [128, 128], "bfloat16"),
-    "VL": ("sbuf", [128, 128], "bfloat16"),
+    "MG": ("sbuf", [128, 16], "float32"),
+    "RM": ("sbuf", [128, 16], "float32"),
+    "D": ("sbuf", [128, 256], "bfloat16"),
+    "SB": ("sbuf", [128, 4 * 512], "bfloat16"),
     "P": ("sbuf", [128, 8 * 256], "bfloat16"),
+    "TT": ("sbuf", [128, 256], "float32"),
     "YS": ("sbuf", [128, 256], "bfloat16"),
-    "S": ("psum", [128, 8 * 256], "float32"),
+    "S": ("psum", [128, 4 * 512], "float32"),
     "X0": ("psum", [128, 512], "float32"),
     "X1": ("psum", [128, 512], "float32"),
-    "X2": ("psum", [128, 512], "float32"),
-    "X3": ("psum", [128, 512], "float32"),
+    "H": ("psum", [128, 512], "float32"),
+    "SV": ("psum", [128, 512], "float32"),
 }
-SEMAPHORES = ["ld_k", "ld_v", "ld_q", "id1", "id2", "mt", "kd", "vd", "kf", "vf", "sent", "ps", "vs", "st"]
+SEMAPHORES = ["ld_k", "ld_v", "ld_q", "mt", "kd", "vd", "kf", "vf", "sent", "ps", "vs", "ac", "gs", "st"]
 
 KCOL = [0, 2, 4, 5, 6, 10, 11, 12]
 VCOL = [1, 3, 7, 8, 9, 13, 14, 15]
+GROUPS = [(0, 1), (1, 1), (2, 3), (5, 3)]
 
 
 def _blk(t, c, n=1):
@@ -71,9 +68,23 @@ def rank_program(g, core, T, topo):
         far_ids.append(DstId(rid=rid, pnc=pid))
     m_rid, m_pid, _se = topo.addr(mate)
 
+    ve, pe, ae = g.vector, g.tensor, g.scalar
+    nv, npe, na = [0], [0], [0]
+
+    def V(ins):
+        ins.then_inc(sem.vs, 1)
+        nv[0] += 1
+        return nv[0]
+
+    def MM(out, lhsT, rhs, start=True, stop=True):
+        pe.matmul(out, lhsT, rhs, start, stop).then_inc(sem.ps, 1)
+        npe[0] += 1
+        return npe[0]
+
     g.sync.dma_start(_blk(KV, KCOL[0]), T.k[:]).then_inc(sem.ld_k, 16)
     g.scalar.dma_start(_blk(KV, VCOL[0]), T.v[:]).then_inc(sem.ld_v, 16)
     g.sync.dma_start(T.Q[:, 0:nb * B], T.q[:, 0:nb * B]).then_inc(sem.ld_q, 16)
+    n_ones = V(ve.memset(T.ONES[:], 1.0))
 
     g.wait_ge(sem.ld_k, 16)
     g.remote_dma_fused([RemoteDMATransfer(
@@ -86,6 +97,8 @@ def rank_program(g, core, T, topo):
         srcs=[_blk(KV, VCOL[0])], dsts=[_blk(KV, VCOL[2] + w) for w in range(nch - 1)], alu_op=0)],
         local_sem=sem.sent)
     g.remote_dma(_blk(KV, KCOL[1], 2), _blk(KV, KCOL[0], 2), sem.mt, sem.sent, m_pid, m_rid, on_mask)
+    g.wait_ge(sem.vs, n_ones)
+    g.affine_select(T.ID[:], T.ONES[:], [[-1, B]], AluOpType.is_equal, 0.0, 0, 1).then_inc(sem.gs, 1)
     n_far = (nch - 1) * n_off
     g.wait_ge(sem.kd, n_far)
     g.remote_dma(_blk(KV, KCOL[5], 3), _blk(KV, KCOL[2], 3), sem.kf, sem.sent, m_pid, m_rid, on_mask)
@@ -93,122 +106,98 @@ def rank_program(g, core, T, topo):
     g.remote_dma(_blk(KV, VCOL[5], 3), _blk(KV, VCOL[2], 3), sem.vf, sem.sent, m_pid, m_rid, on_mask)
     g.wait_ge(sem.sent, 2 * n_off + 3 * n_on)
 
-    ve, pe = g.vector, g.tensor
-    nv, npe = [0], [0]
-
-    def V(ins):
-        ins.then_inc(sem.vs, 1)
-        nv[0] += 1
-        return nv[0]
-
-    def MM(out, lhsT, rhs, start=True, stop=True):
-        pe.matmul(out, lhsT, rhs, start, stop).then_inc(sem.ps, 1)
-        npe[0] += 1
-        return npe[0]
-
-    V(ve.memset(T.IDA[:, 1:129], 0.0))
-    n_ida = V(ve.memset(T.IDA[:, 0:1], -1.0))
-    for c, val in enumerate((0.0, -0.5)):
-        n1 = V(ve.memset(T.SEL[0:2, c * B:(c + 1) * B], val))
-    ve.wait_ge(sem.vs, n1)
-    for c, val in enumerate((-0.5, 0.0)):
-        n_sel = V(ve.memset(T.SEL[0:1, c * B:(c + 1) * B], val))
-    g.scalar.wait_ge(sem.vs, n_ida)
-    g.scalar.dma_start(T.IDD[:], T.IDA[:]).then_inc(sem.id1, 16)
-    g.scalar.wait_ge(sem.id1, 16)
-    g.scalar.dma_start(T.ID[:], T.IDD[0:128, :]).then_inc(sem.id2, 16)
-
     X = [T.X0, T.X1]
-    r_done = {}
+    red_done, cp_done = {}, {}
+    m_ap = [None]
 
-    def scores_t(s):
-        if s >= 2:
-            pe.wait_ge(sem.vs, r_done[s - 2])
+    def group_max(gi):
+        s0, n = GROUPS[gi]
         for b in range(nb):
-            n_st = MM(X[s % 2][:, b * B:(b + 1) * B], _blk(T.Q, b), _blk(KV, KCOL[s]))
-        ve.wait_ge(sem.ps, n_st)
-        if s == 0:
-            r_done[s] = V(ve.tensor_copy(T.R[:, 0:nb * B], X[0][:, 0:nb * B]))
-        else:
-            ve.wait_ge(sem.vs, r_done[s - 1])
-            r_done[s] = V(ve.tensor_tensor(T.R[:, 0:nb * B], X[s % 2][:, 0:nb * B], T.R[:, 0:nb * B],
-                                           AluOpType.max))
+            if gi > 0:
+                pe.wait_ge(sem.vs, red_done[(gi - 1, b)])
+            n_x = MM(X[b][:, 0:n * B], _blk(T.Q, b), _blk(KV, KCOL[s0], n))
+            ve.wait_ge(sem.ps, n_x)
+            red_done[(gi, b)] = V(ve.tensor_reduce(T.MG[:, 2 * gi + b:2 * gi + b + 1], X[b][:, 0:n * B],
+                                                   AxisListType.X, AluOpType.max))
+        if gi == 0:
+            m_ap[0] = T.MG[:, 0:nb]
+            return red_done[(gi, nb - 1)]
+        ve.wait_ge(sem.vs, red_done[(gi, nb - 1)])
+        n_rm = V(ve.tensor_tensor(T.RM[:, 2 * gi:2 * gi + nb], T.MG[:, 2 * gi:2 * gi + nb], m_ap[0], AluOpType.max))
+        m_ap[0] = T.RM[:, 2 * gi:2 * gi + nb]
+        return n_rm
+
+    def scol(s):
+        return (s // 2) * 512 + (s % 2) * W
 
     def scores(s):
-        MM(T.S[:, s * 256:s * 256 + W], _blk(KV, KCOL[s]), T.Q[:, 0:W])
+        n_s = MM(T.S[:, scol(s):scol(s) + W], _blk(KV, KCOL[s]), T.Q[:, 0:W])
+        if s % 2 == 1:
+            c0 = (s // 2) * 512
+            ae.wait_ge(sem.ps, n_s)
+            ae.activation(T.SB[:, c0:c0 + 2 * W], T.S[:, c0:c0 + 2 * W],
+                          ActivationFunctionType.Copy).then_inc(sem.ac, 1)
+            na[0] += 1
+            cp_done[s // 2] = na[0]
 
     def vsum(s):
-        return MM(T.X2[:, 0:B], T.ID[:], _blk(KV, VCOL[s]), s == 0, s == 7)
+        return MM(T.SV[:, 0:1], _blk(KV, VCOL[s]), T.ONES[:, 0:1], s == 0, s == 7)
 
     pe.wait_ge(sem.ld_k, 16)
     pe.wait_ge(sem.ld_q, 16)
-    scores_t(0)
+    group_max(0)
     scores(0)
-    pe.wait_ge(sem.mt, n_on)
-    scores_t(1)
-    scores(1)
-    pe.wait_ge(sem.kd, n_far)
-    for s in (2, 3, 4):
-        scores_t(s)
-    for s in (2, 3, 4):
-        scores(s)
-    pe.wait_ge(sem.id2, 16)
+    pe.wait_ge(sem.vs, n_ones)
     pe.wait_ge(sem.ld_v, 16)
     vsum(0)
+    pe.wait_ge(sem.mt, n_on)
+    group_max(1)
+    scores(1)
     vsum(1)
+    pe.wait_ge(sem.kd, n_far)
+    group_max(2)
+    for s in (2, 3, 4):
+        scores(s)
     pe.wait_ge(sem.kf, n_on)
-    for s in (5, 6, 7):
-        scores_t(s)
+    n_m = group_max(3)
+    scores(5)
+    scores(6)
+
+    ve.wait_ge(sem.gs, 1)
+    ve.wait_ge(sem.vs, n_m)
+    for b in range(nb):
+        wb = min(B, W - b * B)
+        n_d = V(ve.tensor_scalar(T.D[0:wb, b * B:b * B + wb], T.ID[0:wb, 0:wb], m_ap[0][0:wb, b:b + 1], 0.5,
+                                 AluOpType.mult, AluOpType.mult))
+        pe.wait_ge(sem.vs, n_d)
+        n_h = MM(T.H[:, b * B:b * B + wb], T.ONES[0:wb, :], T.D[0:wb, b * B:b * B + wb])
+    scores(7)
     pe.wait_ge(sem.vd, n_far)
     for s in (2, 3, 4):
         vsum(s)
-    for s in (5, 6, 7):
-        scores(s)
-    pe.wait_ge(sem.vf, n_on)
-    for s in (5, 6, 7):
-        n_vs = vsum(s)
 
-    ve.wait_ge(sem.vs, r_done[7])
-    for b in range(nb):
-        n_t = V(ve.tensor_tensor(T.TR[:, b:64 * nb:nb], T.R[:, b * B:b * B + 64], T.R[:, b * B + 64:(b + 1) * B],
-                                 AluOpType.max))
-    off, ln = 0, 64 * nb
-    while ln > nb:
-        h = ln // 2
-        out = T.MT[:, 0:nb] if h == nb else T.TR[:, off + ln:off + ln + h]
-        ve.wait_ge(sem.vs, n_t)
-        n_t = V(ve.tensor_tensor(out, T.TR[:, off:off + h], T.TR[:, off + h:off + ln], AluOpType.max))
-        off, ln = off + ln, h
-
-    pe.wait_ge(sem.vs, n_t)
-    n_m = MM(T.X0[0:nb, 0:B], T.MT[:, 0:nb], T.ID[:])
-    ve.wait_ge(sem.ps, n_vs)
-    n_vh = V(ve.tensor_copy(T.VH[:], T.X2[:, 0:B]))
-    ve.wait_ge(sem.ps, n_m)
-    n_row = V(ve.tensor_copy(T.MROW[0:nb, :], T.X0[0:nb, 0:B]))
-    pe.wait_ge(sem.vs, n_row)
-    for b in range(nb):
-        wb = min(B, W - b * B)
-        n_h = MM(T.X1[:, b * B:b * B + wb], T.SEL[0:nb, b * B:(b + 1) * B], T.MROW[0:nb, 0:wb])
-    ve.wait_ge(sem.vs, n_vh)
-    n_vl = V(ve.tensor_tensor(T.VL[:], T.X2[:, 0:B], T.VH[:], AluOpType.subtract))
     ve.wait_ge(sem.ps, n_h)
-    n_hb = V(ve.tensor_copy(T.HB[:, 0:W], T.X1[:, 0:W]))
-    ve.wait_ge(sem.vs, n_hb)
     p_done = {}
     for s in range(8):
-        p_done[s] = V(ve.tensor_tensor(T.P[:, s * 256:s * 256 + W], T.S[:, s * 256:s * 256 + W], T.HB[:, 0:W],
+        ve.wait_ge(sem.ac, cp_done[s // 2])
+        p_done[s] = V(ve.tensor_tensor(T.P[:, s * 256:s * 256 + W], T.H[:, 0:W], T.SB[:, scol(s):scol(s) + W],
                                        AluOpType.max))
 
-    Y = T.X3[:, 0:W]
-    pe.wait_ge(sem.vs, n_hb)
-    MM(Y, T.VH[:], T.HB[:, 0:W], True, False)
-    MM(Y, T.VL[:], T.HB[:, 0:W], False, False)
+    Y = T.S[:, 0:W]
+    pe.wait_ge(sem.ac, cp_done[0])
+    n_sv = 0
     for s in range(8):
+        if s == 5:
+            pe.wait_ge(sem.vf, n_on)
+            for s2 in (5, 6, 7):
+                n_sv = vsum(s2)
         pe.wait_ge(sem.vs, p_done[s])
-        n_y = MM(Y, _blk(KV, VCOL[s]), T.P[:, s * 256:s * 256 + W], False, s == 7)
+        n_y = MM(Y, _blk(KV, VCOL[s]), T.P[:, s * 256:s * 256 + W], s == 0, s == 7)
+    ve.wait_ge(sem.ps, n_sv)
+    n_t = V(ve.tensor_scalar(T.TT[:, 0:W], T.H[:, 0:W], T.SV[:, 0:1], None, AluOpType.mult))
     ve.wait_ge(sem.ps, n_y)
-    n_out = V(ve.tensor_copy(T.YS[:, 0:W], Y))
+    ve.wait_ge(sem.vs, n_t)
+    n_out = V(ve.tensor_tensor(T.YS[:, 0:W], Y, T.TT[:, 0:W], AluOpType.subtract))
     g.sync.wait_ge(sem.vs, n_out)
     g.sync.dma_start(T.y[:, 0:W], T.YS[:, 0:W]).then_inc(sem.st, 16)
     g.sync.wait_ge(sem.st, 16)

from concourse.bass import DstId, RemoteDMATransfer
from concourse.mybir import AluOpType, AxisListType, ActivationFunctionType

B = 128
SCRATCH = {
    "KV": ("sbuf", [128, 16 * B], "bfloat16"),
    "Q": ("sbuf", [128, 256], "bfloat16"),
    "ONES": ("sbuf", [128, 128], "bfloat16"),
    "ID": ("sbuf", [128, 128], "bfloat16"),
    "MG": ("sbuf", [128, 16], "float32"),
    "RM": ("sbuf", [128, 16], "float32"),
    "D": ("sbuf", [128, 256], "bfloat16"),
    "SB": ("sbuf", [128, 4 * 512], "bfloat16"),
    "P": ("sbuf", [128, 8 * 256], "bfloat16"),
    "TT": ("sbuf", [128, 256], "float32"),
    "YS": ("sbuf", [128, 256], "bfloat16"),
    "S": ("psum", [128, 4 * 512], "float32"),
    "X0": ("psum", [128, 512], "float32"),
    "X1": ("psum", [128, 512], "float32"),
    "H": ("psum", [128, 512], "float32"),
    "SV": ("psum", [128, 512], "float32"),
}
SEMAPHORES = ["ld_k", "ld_v", "ld_q", "mt", "kd", "vd", "kf", "vf", "sent", "ps", "vs", "ac", "gs", "st"]

KCOL = [0, 2, 4, 5, 6, 10, 11, 12]
VCOL = [1, 3, 7, 8, 9, 13, 14, 15]
GROUPS = [(0, 1), (1, 1), (2, 3), (5, 3)]


def _blk(t, c, n=1):
    return t[:, c * B:(c + n) * B]


def _bits(m):
    return bin(m).count("1")


def rank_program(g, core, T, topo):
    rank = T.rank_of(core)
    if rank is None:
        return
    W = T.tables["WID"][rank]
    nb = (W + B - 1) // B
    sem = T.sem
    KV = T.KV

    chips, members = [], {}
    for c in T.cores:
        ch = topo.chip(c)
        if ch not in members:
            chips.append(ch)
            members[ch] = []
        members[ch].append(c)
    nch = len(chips)
    ci = chips.index(topo.chip(core))
    pos = members[chips[ci]].index(core)
    mate = members[chips[ci]][1 - pos]
    far = [members[chips[(ci + w) % nch]][pos] for w in range(1, nch)]
    off_mask = topo.mask(core, mate)
    for d in far:
        assert topo.may_write(core, d)
        off_mask &= topo.mask(core, d)
    on_mask = topo.mask(core, mate) & ~off_mask
    n_off, n_on = _bits(off_mask), _bits(on_mask)
    far_ids = []
    for d in far:
        rid, pid, _se = topo.addr(d)
        far_ids.append(DstId(rid=rid, pnc=pid))
    m_rid, m_pid, _se = topo.addr(mate)

    ve, pe, ae = g.vector, g.tensor, g.scalar
    nv, npe, na = [0], [0], [0]

    def V(ins):
        ins.then_inc(sem.vs, 1)
        nv[0] += 1
        return nv[0]

    def MM(out, lhsT, rhs, start=True, stop=True):
        pe.matmul(out, lhsT, rhs, start, stop).then_inc(sem.ps, 1)
        npe[0] += 1
        return npe[0]

    g.sync.dma_start(_blk(KV, KCOL[0]), T.k[:]).then_inc(sem.ld_k, 16)
    g.scalar.dma_start(_blk(KV, VCOL[0]), T.v[:]).then_inc(sem.ld_v, 16)
    g.sync.dma_start(T.Q[:, 0:nb * B], T.q[:, 0:nb * B]).then_inc(sem.ld_q, 16)
    n_ones = V(ve.memset(T.ONES[:], 1.0))

    g.wait_ge(sem.ld_k, 16)
    g.remote_dma_fused([RemoteDMATransfer(
        dst_ids=far_ids, dma_engine_mask=off_mask, remote_sem=sem.kd,
        srcs=[_blk(KV, KCOL[0])], dsts=[_blk(KV, KCOL[2] + w) for w in range(nch - 1)], alu_op=0)],
        local_sem=sem.sent)
    g.wait_ge(sem.ld_v, 16)
    g.remote_dma_fused([RemoteDMATransfer(
        dst_ids=far_ids, dma_engine_mask=off_mask, remote_sem=sem.vd,
        srcs=[_blk(KV, VCOL[0])], dsts=[_blk(KV, VCOL[2] + w) for w in range(nch - 1)], alu_op=0)],
        local_sem=sem.sent)
    g.remote_dma(_blk(KV, KCOL[1], 2), _blk(KV, KCOL[0], 2), sem.mt, sem.sent, m_pid, m_rid, on_mask)
    g.wait_ge(sem.vs, n_ones)
    g.affine_select(T.ID[:], T.ONES[:], [[-1, B]], AluOpType.is_equal, 0.0, 0, 1).then_inc(sem.gs, 1)
    n_far = (nch - 1) * n_off
    g.wait_ge(sem.kd, n_far)
    g.remote_dma(_blk(KV, KCOL[5], 3), _blk(KV, KCOL[2], 3), sem.kf, sem.sent, m_pid, m_rid, on_mask)
    g.wait_ge(sem.vd, n_far)
    g.remote_dma(_blk(KV, VCOL[5], 3), _blk(KV, VCOL[2], 3), sem.vf, sem.sent, m_pid, m_rid, on_mask)
    g.wait_ge(sem.sent, 2 * n_off + 3 * n_on)

    X = [T.X0, T.X1]
    red_done, cp_done = {}, {}
    m_ap = [None]

    def group_max(gi):
        s0, n = GROUPS[gi]
        for b in range(nb):
            if gi > 0:
                pe.wait_ge(sem.vs, red_done[(gi - 1, b)])
            n_x = MM(X[b][:, 0:n * B], _blk(T.Q, b), _blk(KV, KCOL[s0], n))
            ve.wait_ge(sem.ps, n_x)
            red_done[(gi, b)] = V(ve.tensor_reduce(T.MG[:, 2 * gi + b:2 * gi + b + 1], X[b][:, 0:n * B],
                                                   AxisListType.X, AluOpType.max))
        if gi == 0:
            m_ap[0] = T.MG[:, 0:nb]
            return red_done[(gi, nb - 1)]
        ve.wait_ge(sem.vs, red_done[(gi, nb - 1)])
        n_rm = V(ve.tensor_tensor(T.RM[:, 2 * gi:2 * gi + nb], T.MG[:, 2 * gi:2 * gi + nb], m_ap[0], AluOpType.max))
        m_ap[0] = T.RM[:, 2 * gi:2 * gi + nb]
        return n_rm

    def scol(s):
        return (s // 2) * 512 + (s % 2) * W

    def scores(s):
        n_s = MM(T.S[:, scol(s):scol(s) + W], _blk(KV, KCOL[s]), T.Q[:, 0:W])
        if s % 2 == 1:
            c0 = (s // 2) * 512
            ae.wait_ge(sem.ps, n_s)
            ae.activation(T.SB[:, c0:c0 + 2 * W], T.S[:, c0:c0 + 2 * W],
                          ActivationFunctionType.Copy).then_inc(sem.ac, 1)
            na[0] += 1
            cp_done[s // 2] = na[0]

    def vsum(s):
        return MM(T.SV[:, 0:1], _blk(KV, VCOL[s]), T.ONES[:, 0:1], s == 0, s == 7)

    pe.wait_ge(sem.ld_k, 16)
    pe.wait_ge(sem.ld_q, 16)
    group_max(0)
    scores(0)
    pe.wait_ge(sem.vs, n_ones)
    pe.wait_ge(sem.ld_v, 16)
    vsum(0)
    pe.wait_ge(sem.mt, n_on)
    group_max(1)
    scores(1)
    vsum(1)
    pe.wait_ge(sem.kd, n_far)
    group_max(2)
    for s in (2, 3, 4):
        scores(s)
    pe.wait_ge(sem.kf, n_on)
    n_m = group_max(3)
    scores(5)
    scores(6)

    ve.wait_ge(sem.gs, 1)
    ve.wait_ge(sem.vs, n_m)
    for b in range(nb):
        wb = min(B, W - b * B)
        n_d = V(ve.tensor_scalar(T.D[0:wb, b * B:b * B + wb], T.ID[0:wb, 0:wb], m_ap[0][0:wb, b:b + 1], 0.5,
                                 AluOpType.mult, AluOpType.mult))
        pe.wait_ge(sem.vs, n_d)
        n_h = MM(T.H[:, b * B:b * B + wb], T.ONES[0:wb, :], T.D[0:wb, b * B:b * B + wb])
    scores(7)
    pe.wait_ge(sem.vd, n_far)
    for s in (2, 3, 4):
        vsum(s)

    ve.wait_ge(sem.ps, n_h)
    p_done = {}
    for s in range(8):
        ve.wait_ge(sem.ac, cp_done[s // 2])
        p_done[s] = V(ve.tensor_tensor(T.P[:, s * 256:s * 256 + W], T.H[:, 0:W], T.SB[:, scol(s):scol(s) + W],
                                       AluOpType.max))

    Y = T.S[:, 0:W]
    pe.wait_ge(sem.ac, cp_done[0])
    n_sv = 0
    for s in range(8):
        if s == 5:
            pe.wait_ge(sem.vf, n_on)
            for s2 in (5, 6, 7):
                n_sv = vsum(s2)
        pe.wait_ge(sem.vs, p_done[s])
        n_y = MM(Y, _blk(KV, VCOL[s]), T.P[:, s * 256:s * 256 + W], s == 0, s == 7)
    ve.wait_ge(sem.ps, n_sv)
    n_t = V(ve.tensor_scalar(T.TT[:, 0:W], T.H[:, 0:W], T.SV[:, 0:1], None, AluOpType.mult))
    ve.wait_ge(sem.ps, n_y)
    ve.wait_ge(sem.vs, n_t)
    n_out = V(ve.tensor_tensor(T.YS[:, 0:W], Y, T.TT[:, 0:W], AluOpType.subtract))
    g.sync.wait_ge(sem.vs, n_out)
    g.sync.dma_start(T.y[:, 0:W], T.YS[:, 0:W]).then_inc(sem.st, 16)
    g.sync.wait_ge(sem.st, 16)
